import numpy as np
import ml_dtypes


def mxq(x, axis, fmt="e4m3"):
    dtype, down = {"e4m3": (ml_dtypes.float8_e4m3fn, 7), "e5m2": (ml_dtypes.float8_e5m2, 14)}[fmt]
    v = np.moveaxis(np.asarray(x, np.float32).astype(ml_dtypes.bfloat16).astype(np.float64), axis, -1)
    blocks = v.reshape(v.shape[:-1] + (-1, 32))
    amax = np.abs(blocks).max(-1, keepdims=True)
    byte = np.maximum(np.where(amax > 0, np.frexp(amax)[1] - 1 + 127, 0) - down, 1)
    scale = np.exp2(byte - 127.0)
    codes = (blocks / scale).astype(np.float32).astype(dtype).astype(np.float64)
    return np.moveaxis((codes * scale).reshape(v.shape), -1, axis)


WIDE = False


def mx_kscale(k):
    if not WIDE:
        return np.ones(k)
    levels = np.array([10, -10, 5, -5, 0])
    if k % 512:
        return np.exp2(np.random.permutation(np.resize(levels, k // 32))).repeat(32)
    a = np.empty((k // 512, 16))
    for p in range(k // 512):
        a[p, :8] = np.random.permutation(np.resize(levels, 8))
        for g in range(8):
            far = levels[np.abs(levels - a[p, g]) >= 10]
            a[p, g + 8] = far[np.random.randint(len(far))]
    return np.exp2(a.ravel()).repeat(32)


def f64(x):
    return np.asarray(x).astype(np.float64)


def striped(idx):
    return np.tile(idx.reshape(-1, 16).T, (8, 1)).astype(np.uint16)


def unstriped(offs):
    return offs[:16].T.reshape(-1).astype(np.int64)


def striped8(idx):
    return np.concatenate([x.reshape(-1, 16).T for x in idx]).astype(np.uint16)


def runs(offs, k):
    lists = np.stack([offs[16 * r : 16 * r + 16].T.reshape(-1) for r in range(8)]).astype(np.int64)
    return lists[np.arange(k) % 512 // 64]


def pack_weight(w):
    k, n = w.shape
    w = f64(np.asarray(w, np.float32).astype(ml_dtypes.bfloat16)).reshape(k // 32, 32, n)
    amax = np.abs(w).max(1)
    byte = np.clip(np.where(amax > 0, np.frexp(amax)[1] - 1 + 127 - 7, 1), 1, 254)
    scaled = (w * np.exp2(127.0 - byte)[:, None, :]).reshape(k, n).astype(np.float32)
    words = np.ascontiguousarray(scaled.reshape(k // 512, 128, 4, n).transpose(0, 1, 3, 2)).astype(ml_dtypes.float8_e4m3fn).view(np.uint8)
    return words, np.ascontiguousarray(byte.astype(np.uint8).reshape(k // 512, 16, n))


def unpack_weight(words, scales):
    g, p, n, _ = words.shape
    vals = np.ascontiguousarray(words).view(ml_dtypes.float8_e4m3fn).astype(np.float64) * np.repeat(np.exp2(scales.astype(np.float64) - 127.0), 8, axis=1)[..., None]
    return vals.transpose(0, 1, 3, 2).reshape(g * 512, n)


def sigmoid(v):
    return 1.0 / (1.0 + np.exp(-np.maximum(v, -700.0)))


K, T, S, N, H = 512, 2048, 512, 512, 512


def setup_inputs():
    n = np.random.standard_normal
    s = mx_kscale(K)[:, None]
    u = mx_kscale(S)
    packed_xT = pack_weight(n((K, T)) * s)
    return {
        "x_words": packed_xT[0],
        "x_scales": packed_xT[1],
        "wa": (n((K, H)) / np.sqrt(K) / s).astype(np.float32),
        "wb": (n((K, N)) / np.sqrt(K) / s).astype(np.float32),
        "gt": (np.random.uniform(0.5, 1.5, (S, 1)) * u[:, None]).astype(np.float32),
        "gi": (np.random.uniform(0.5, 1.5, (S, 1)) / u[:, None]).astype(np.float32),
        "offs": striped(np.random.permutation(T)[:S]),
        "two": striped(np.random.permutation(T)[:S]),
        "n1": striped8(np.stack([np.random.permutation(H) for _ in range(8)])),
        "n2": striped8(np.stack([np.random.permutation(H) for _ in range(8)])),
        "n3": striped8(np.stack([np.random.permutation(H) for _ in range(8)])),
        "n4": striped8(np.stack([np.random.permutation(N) for _ in range(8)])),
        "n5": striped8(np.stack([np.random.permutation(N) for _ in range(8)])),
    }


def reference(x_words, x_scales, wa, wb, gt, gi, offs, two, n1, n2, n3, n4, n5):
    xq = unpack_weight(x_words, x_scales)[:, unstriped(offs)]
    a = xq.T @ mxq(f64(wa), 0, "e4m3")
    pa = a[np.arange(S)[:, None], runs(n1, S)]
    z = f64(gt) * (pa + (sigmoid(a[np.arange(S)[:, None], runs(n2, S)])) * (a[np.arange(S)[:, None], runs(n3, S)] - pa))
    x_two = unpack_weight(x_words, x_scales)[:, unstriped(two)]
    b = x_two.T @ mxq(f64(wb), 0, "e4m3")
    z2 = f64(gi) * b
    cv = 0.0625 * ((mxq(z, 0, "e4m3").T @ mxq(z2, 0, "e4m3")))
    return np.maximum(cv * (sigmoid(cv[np.arange(H)[:, None], runs(n4, H)])), cv[np.arange(H)[:, None], runs(n5, H)])

@@ -1,0 +1,210 @@
+from contextlib import ExitStack
+
+import concourse.mybir as mybir
+
+K, T, S, H, N = 512, 2048, 512, 512, 512
+FLOPS = 2 * K * S * H + 2 * K * S * N + 2 * S * H * N
+
+F32 = mybir.dt.float32
+BF16 = mybir.dt.bfloat16
+I32 = mybir.dt.int32
+U32 = mybir.dt.uint32
+U16 = mybir.dt.uint16
+U8 = mybir.dt.uint8
+FP8X4 = mybir.dt.float8_e4m3fn_x4
+ALU = mybir.AluOpType
+ACT = mybir.ActivationFunctionType
+
+P = 128
+PACK = 4
+HALF = 256
+
+
+def tile_picked_momlerpgmax_none_p_kernel(
+    tc, x_words, x_scales, wa, wb, gt, gi, offs, two, n1, n2, n3, n4, n5, out
+):
+    nc = tc.nc
+    with ExitStack() as ctx:
+        keep = ctx.enter_context(tc.tile_pool(name="keep", bufs=1))
+        psum = ctx.enter_context(tc.psum_pool(name="psum", bufs=1))
+
+        def load_list(name, src):
+            tile = keep.tile([P, S // 16], U16, name=name)
+            nc.sync.dma_start(tile[:], src)
+            return tile
+
+        def load_weight_half(name, w, half):
+            raw = keep.tile([P, PACK, HALF], F32, name=name)
+            nc.sync.dma_start(
+                raw[:], w.rearrange("(p j) c -> p j c", j=PACK)[:, :, half * HALF : (half + 1) * HALF]
+            )
+            return raw
+
+        def load_gain(name, g):
+            tile = keep.tile([P, PACK], F32, name=name)
+            nc.sync.dma_start(tile[:], g.rearrange("(p t) o -> p (t o)", t=PACK))
+            return tile
+
+        def interleave(copy, dst, src):
+            copy(
+                dst.rearrange("p (c i t) -> p c t i", i=4, t=PACK),
+                src.rearrange("p t (c i) -> p c t i", i=4),
+            )
+
+        def quantise(codes, scales, grouped):
+            nc.vector.quantize_mx(out=codes.bitcast(FP8X4), scales=scales, in_=grouped)
+
+        def product(acc, l_codes, l_scales, r_codes, r_scales):
+            nc.tensor.matmul_mx(
+                out=acc,
+                lhsT=l_codes.bitcast(FP8X4),
+                lhsT_scale=l_scales,
+                rhs=r_codes.bitcast(FP8X4),
+                rhs_scale=r_scales,
+                start=True,
+                stop=True,
+            )
+
+        plane = keep.tile([P, T], U8, name="plane", align_bytes=64)
+        nc.vector.memset(plane[:].bitcast(I32), 0)
+        warm = keep.tile([P, 1], F32, name="warm")
+        warm_out = keep.tile([P, 1], F32, name="warm_out")
+        nc.gpsimd.memset(warm[:], 0.0)
+        nc.scalar.activation(warm_out[:], warm[:], ACT.Sigmoid)
+        rows = [keep.tile([P, 2 * H], F32, name=f"rows{t}") for t in range(PACK)]
+        for t in range(PACK):
+            nc.vector.memset(rows[t][:, H:], 0.0)
+
+        offs_t = load_list("offs_t", offs)
+        for q in range(4):
+            nc.sync.dma_start(
+                plane[32 * q : 32 * q + 4, :].bitcast(I32), x_scales[0, 4 * q : 4 * q + 4, :].bitcast(I32)
+            )
+        wa_raw = [load_weight_half(f"wa_raw{h}", wa, h) for h in range(2)]
+        words = keep.tile([P, T], I32, name="words")
+        nc.sync.dma_start(words[:], x_words[0].rearrange("p c r -> p (c r)").bitcast(I32))
+        two_t = load_list("two_t", two)
+        n2_t = load_list("n2_t", n2)
+        n3_t = load_list("n3_t", n3)
+        n1_t = load_list("n1_t", n1)
+        gt_t = load_gain("gt_t", gt)
+        wb_raw = [load_weight_half(f"wb_raw{h}", wb, h) for h in range(2)]
+        gi_t = load_gain("gi_t", gi)
+        n5_t = load_list("n5_t", n5)
+        n4_t = load_list("n4_t", n4)
+
+        def pick_scales(name, idx):
+            picked = keep.tile([P, S], U8, name=name + "_picked", align_bytes=64)
+            nc.vector.tensor_copy(picked[:], plane[:].indirect(idx[:]))
+            dealt = keep.tile([P, S], U8, name=name + "_dealt", align_bytes=64)
+            nc.vector.tensor_copy(
+                dealt[:].rearrange("p (t m) -> p m t", t=PACK), picked[:].rearrange("p (m t) -> p m t", t=PACK)
+            )
+            return dealt
+
+        def pick_words(name, idx):
+            dealt = keep.tile([P, S], U32, name=name, align_bytes=64)
+            nc.vector.tensor_copy(
+                dealt[:].rearrange("p (t m) -> p m t", t=PACK), words[:].bitcast(U32).indirect(idx[:])
+            )
+            return dealt
+
+        def weight_operand(name, raws):
+            codes = keep.tile([P, H], U32, name=name + "_codes", align_bytes=64)
+            scales = keep.tile([P, H], U8, name=name + "_scales", align_bytes=64)
+            for h in range(2):
+                grouped = keep.tile([P, PACK * HALF], BF16, name=f"{name}_grouped{h}", align_bytes=64)
+                interleave(nc.scalar.copy, grouped[:], raws[h][:])
+                cols = slice(h * HALF, (h + 1) * HALF)
+                quantise(codes[:, cols], scales[:, cols], grouped[:])
+            return codes, scales
+
+        xa_scales = pick_scales("xa_scales", offs_t)
+        wa_codes, wa_scales = weight_operand("wa", wa_raw)
+        xa_codes = pick_words("xa_codes", offs_t)
+        a_banks = [psum.tile([P, H], F32, name=f"a_bank{t}", tag=f"bank{t}") for t in range(PACK)]
+        for t in range(PACK):
+            cols = slice(t * P, (t + 1) * P)
+            product(a_banks[t][:], xa_codes[:, cols], xa_scales[:, cols], wa_codes[:], wa_scales[:])
+        xb_scales = pick_scales("xb_scales", two_t)
+        xb_codes = pick_words("xb_codes", two_t)
+
+        neg_gt = keep.tile([P, PACK], F32, name="neg_gt")
+        nc.scalar.mul(neg_gt[:], gt_t[:], -1.0)
+
+        z_planes = keep.tile([P, PACK, H], BF16, name="z_planes", align_bytes=64)
+        z2_planes = keep.tile([P, PACK, N], BF16, name="z2_planes", align_bytes=64)
+
+        def mix(t):
+            nc.scalar.copy(rows[t][:, :H], a_banks[t][:])
+            gate = keep.tile([P, H], F32, name=f"gate{t}")
+            nc.scalar.activation(gate[:], rows[t][:].indirect(n2_t[:]), ACT.Sigmoid)
+            rest = keep.tile([P, H], F32, name=f"rest{t}")
+            nc.scalar.activation(
+                rest[:], gate[:], ACT.Identity, bias=gt_t[:, t : t + 1], scale=neg_gt[:, t : t + 1]
+            )
+            far = keep.tile([P, H], F32, name=f"far{t}")
+            nc.vector.tensor_tensor(far[:], rows[t][:].indirect(n3_t[:]), gate[:], ALU.mult)
+            near = keep.tile([P, H], F32, name=f"near{t}")
+            nc.vector.tensor_tensor(near[:], rows[t][:].indirect(n1_t[:]), rest[:], ALU.mult)
+            return far, near
+
+        def join(t, far, near):
+            nc.vector.scalar_tensor_tensor(
+                z_planes[:, t, :].rearrange("p (u m) -> p m u", u=PACK),
+                far[:].rearrange("p (m u) -> p m u", u=PACK),
+                gt_t[:, t : t + 1],
+                near[:].rearrange("p (m u) -> p m u", u=PACK),
+                ALU.mult,
+                ALU.add,
+            )
+
+        parts0 = mix(0)
+        parts1 = mix(1)
+        join(0, *parts0)
+        wb_codes, wb_scales = weight_operand("wb", wb_raw)
+        b_banks = [psum.tile([P, N], F32, name=f"b_bank{t}") for t in range(PACK)]
+        for t in range(PACK):
+            cols = slice(t * P, (t + 1) * P)
+            product(b_banks[t][:], xb_codes[:, cols], xb_scales[:, cols], wb_codes[:], wb_scales[:])
+        parts2 = mix(2)
+        join(1, *parts1)
+        parts3 = mix(3)
+        join(2, *parts2)
+        for t in range(PACK):
+            nc.scalar.activation(z2_planes[:, t, :], b_banks[t][:], ACT.Copy, scale=gi_t[:, t : t + 1])
+        z2_grouped = keep.tile([P, PACK * N], BF16, name="z2_grouped", align_bytes=64)
+        interleave(nc.vector.tensor_copy, z2_grouped[:], z2_planes[:])
+        join(3, *parts3)
+        z2_codes = keep.tile([P, N], U32, name="z2_codes", align_bytes=64)
+        z2_scales = keep.tile([P, N], U8, name="z2_scales", align_bytes=64)
+        quantise(z2_codes[:], z2_scales[:], z2_grouped[:])
+
+        z_grouped = [keep.tile([P, PACK * P], BF16, name=f"z_grouped{u}", align_bytes=64) for u in range(PACK)]
+        z_codes = [keep.tile([P, P], U32, name=f"z_codes{u}", align_bytes=64) for u in range(PACK)]
+        z_scales = [keep.tile([P, P], U8, name=f"z_scales{u}", align_bytes=64) for u in range(PACK)]
+        cv_banks = [psum.tile([P, N], F32, name=f"cv_bank{u}", tag=f"bank{u}") for u in range(PACK)]
+        for u in range(PACK + 1):
+            if u < PACK:
+                interleave(nc.vector.tensor_copy, z_grouped[u][:], z_planes[:, :, u * P : (u + 1) * P])
+            if u > 0:
+                quantise(z_codes[u - 1][:], z_scales[u - 1][:], z_grouped[u - 1][:])
+                product(cv_banks[u - 1][:], z_codes[u - 1][:], z_scales[u - 1][:], z2_codes[:], z2_scales[:])
+
+        out_rows = out.rearrange("(p u) n -> p u n", u=PACK)
+        gated = []
+        other = []
+        for u in range(PACK + 1):
+            if u < PACK:
+                nc.scalar.activation(rows[u][:, :N], cv_banks[u][:], ACT.Copy, scale=0.0625)
+                gate = keep.tile([P, N], F32, name=f"cv_gate{u}")
+                nc.scalar.activation(gate[:], rows[u][:].indirect(n4_t[:]), ACT.Sigmoid)
+                other.append(keep.tile([P, N], F32, name=f"other{u}"))
+                nc.vector.tensor_copy(other[u][:], rows[u][:].indirect(n5_t[:]))
+            if u > 0:
+                result = keep.tile([P, N], F32, name=f"result{u - 1}")
+                nc.vector.tensor_tensor(result[:], gated[u - 1][:], other[u - 1][:], ALU.max)
+                nc.sync.dma_start(out_rows[:, u - 1, :], result[:])
+            if u < PACK:
+                gated.append(keep.tile([P, N], F32, name=f"gated{u}"))
+                nc.vector.tensor_tensor(gated[u][:], rows[u][:, :N], gate[:], ALU.mult)

@@ -1,6 +1,7 @@
 from contextlib import ExitStack
 
 import concourse.mybir as mybir
+from concourse.masks import make_identity
 
 K, T, S, H, N = 512, 2048, 512, 512, 512
 FLOPS = 2 * K * S * H + 2 * K * S * N + 2 * S * H * N
@@ -18,6 +19,8 @@ ACT = mybir.ActivationFunctionType
 P = 128
 PACK = 4
 HALF = 256
+WA_PIECES = ((0, 256), (256, 384), (384, 512))
+WB_PIECES = ((0, 256), (256, 512))
 
 
 def tile_picked_momlerpgmax_none_p_kernel(
@@ -33,17 +36,19 @@ def tile_picked_momlerpgmax_none_p_kernel(
             nc.sync.dma_start(tile[:], src)
             return tile
 
-        def load_weight_half(name, w, half):
-            raw = keep.tile([P, PACK, HALF], F32, name=name)
-            nc.sync.dma_start(
-                raw[:], w.rearrange("(p j) c -> p j c", j=PACK)[:, :, half * HALF : (half + 1) * HALF]
-            )
-            return raw
+        def load_weight(name, w, pieces):
+            raws = []
+            for lo, hi in pieces:
+                raw = keep.tile([P, PACK, hi - lo], F32, name=f"{name}{lo}", tag=f"{name}{lo}", align_bytes=64)
+                nc.sync.dma_start(raw[:], w.rearrange("(p j) c -> p j c", j=PACK)[:, :, lo:hi])
+                raws.append(raw)
+            return raws
 
-        def load_gain(name, g):
-            tile = keep.tile([P, PACK], F32, name=name)
-            nc.sync.dma_start(tile[:], g.rearrange("(p t) o -> p (t o)", t=PACK))
-            return tile
+        def load_gain(first_row, g):
+            nc.sync.dma_start(
+                gain_rows[first_row : first_row + PACK, :].rearrange("t (b q) -> t b q", q=8),
+                g.rearrange("(b t q) o -> t b (q o)", t=PACK, q=8),
+            )
 
         def interleave(copy, dst, src):
             copy(
@@ -66,11 +71,15 @@ def tile_picked_momlerpgmax_none_p_kernel(
             )
 
         plane = keep.tile([P, T], U8, name="plane", align_bytes=64)
-        nc.vector.memset(plane[:].bitcast(I32), 0)
+        nc.gpsimd.memset(plane[:].bitcast(I32), 0)
         warm = keep.tile([P, 1], F32, name="warm")
         warm_out = keep.tile([P, 1], F32, name="warm_out")
         nc.gpsimd.memset(warm[:], 0.0)
         nc.scalar.activation(warm_out[:], warm[:], ACT.Sigmoid)
+        gain_rows = keep.tile([P, P], F32, name="gain_rows")
+        nc.gpsimd.memset(gain_rows[:], 0.0)
+        identity = keep.tile([P, P], F32, name="identity")
+        make_identity(nc, identity[:])
         rows = [keep.tile([P, 2 * H], F32, name=f"rows{t}") for t in range(PACK)]
         for t in range(PACK):
             nc.vector.memset(rows[t][:, H:], 0.0)
@@ -80,16 +89,16 @@ def tile_picked_momlerpgmax_none_p_kernel(
             nc.sync.dma_start(
                 plane[32 * q : 32 * q + 4, :].bitcast(I32), x_scales[0, 4 * q : 4 * q + 4, :].bitcast(I32)
             )
-        wa_raw = [load_weight_half(f"wa_raw{h}", wa, h) for h in range(2)]
+        two_t = load_list("two_t", two)
         words = keep.tile([P, T], I32, name="words")
         nc.sync.dma_start(words[:], x_words[0].rearrange("p c r -> p (c r)").bitcast(I32))
-        two_t = load_list("two_t", two)
+        wa_raw = load_weight("wa_raw", wa, WA_PIECES)
+        load_gain(0, gt)
+        load_gain(PACK, gi)
         n2_t = load_list("n2_t", n2)
         n3_t = load_list("n3_t", n3)
         n1_t = load_list("n1_t", n1)
-        gt_t = load_gain("gt_t", gt)
-        wb_raw = [load_weight_half(f"wb_raw{h}", wb, h) for h in range(2)]
-        gi_t = load_gain("gi_t", gi)
+        wb_raw = load_weight("wb_raw", wb, WB_PIECES)
         n5_t = load_list("n5_t", n5)
         n4_t = load_list("n4_t", n4)
 
@@ -98,87 +107,115 @@ def tile_picked_momlerpgmax_none_p_kernel(
             nc.vector.tensor_copy(picked[:], plane[:].indirect(idx[:]))
             dealt = keep.tile([P, S], U8, name=name + "_dealt", align_bytes=64)
             nc.vector.tensor_copy(
-                dealt[:].rearrange("p (t m) -> p m t", t=PACK), picked[:].rearrange("p (m t) -> p m t", t=PACK)
+                dealt[:].bitcast(I32).rearrange("p (t b w) -> p t b w", t=PACK, w=2),
+                picked[:].bitcast(I32).rearrange("p (b t w) -> p t b w", t=PACK, w=2),
             )
             return dealt
 
-        def pick_words(name, idx):
-            dealt = keep.tile([P, S], U32, name=name, align_bytes=64)
+        def pick_words(name, idx, tag):
+            dealt = keep.tile([P, S], U32, name=name, tag=tag, align_bytes=64)
             nc.vector.tensor_copy(
-                dealt[:].rearrange("p (t m) -> p m t", t=PACK), words[:].bitcast(U32).indirect(idx[:])
+                dealt[:].rearrange("p (t b q) -> p b t q", t=PACK, q=8), words[:].bitcast(U32).indirect(idx[:])
             )
             return dealt
 
-        def weight_operand(name, raws):
+        def operand_tiles(name):
             codes = keep.tile([P, H], U32, name=name + "_codes", align_bytes=64)
             scales = keep.tile([P, H], U8, name=name + "_scales", align_bytes=64)
-            for h in range(2):
-                grouped = keep.tile([P, PACK * HALF], BF16, name=f"{name}_grouped{h}", align_bytes=64)
-                interleave(nc.scalar.copy, grouped[:], raws[h][:])
-                cols = slice(h * HALF, (h + 1) * HALF)
-                quantise(codes[:, cols], scales[:, cols], grouped[:])
             return codes, scales
 
+        def group_piece(name, copy, source):
+            grouped = keep.tile([P, PACK * source.shape[2]], BF16, name=name, align_bytes=64)
+            interleave(copy, grouped[:], source)
+            return grouped
+
+        def quantise_piece(operand, piece, grouped):
+            lo, hi = piece
+            quantise(operand[0][:, lo:hi], operand[1][:, lo:hi], grouped[:])
+
+        on_scalar, on_vector = nc.scalar.copy, nc.vector.tensor_copy
         xa_scales = pick_scales("xa_scales", offs_t)
-        wa_codes, wa_scales = weight_operand("wa", wa_raw)
-        xa_codes = pick_words("xa_codes", offs_t)
+        xb_scales = pick_scales("xb_scales", two_t)
+        xa_codes = pick_words("xa_codes", offs_t, "xa_codes")
+        wa_op = operand_tiles("wa")
+        wa_grouped = [
+            group_piece(f"wa_grouped{i}", copy, wa_raw[i][:]) for i, copy in enumerate((on_scalar, on_vector, on_vector))
+        ]
+        for piece, grouped in zip(WA_PIECES, wa_grouped):
+            quantise_piece(wa_op, piece, grouped)
+
+        gain_bank = psum.tile([P, P], F32, name="gain_bank", tag="bank7")
+        nc.tensor.transpose(gain_bank[:], gain_rows[:], identity[:])
+        gains = keep.tile([P, 2 * PACK], F32, name="gains")
+        nc.scalar.copy(gains[:], gain_bank[:, : 2 * PACK])
+        neg_gt = keep.tile([P, PACK], F32, name="neg_gt")
+        nc.scalar.mul(neg_gt[:], gain_bank[:, :PACK], -1.0)
+        gt_t = gains[:, :PACK]
+        gi_t = gains[:, PACK:]
+
+        a_first = psum.tile([P, HALF], F32, name="a_first", tag="bank4")
+        product(a_first[:], xa_codes[:, :P], xa_scales[:, :P], wa_op[0][:, :HALF], wa_op[1][:, :HALF])
+        nc.scalar.copy(rows[0][:, :HALF], a_first[:])
         a_banks = [psum.tile([P, H], F32, name=f"a_bank{t}", tag=f"bank{t}") for t in range(PACK)]
         for t in range(PACK):
             cols = slice(t * P, (t + 1) * P)
-            product(a_banks[t][:], xa_codes[:, cols], xa_scales[:, cols], wa_codes[:], wa_scales[:])
-        xb_scales = pick_scales("xb_scales", two_t)
-        xb_codes = pick_words("xb_codes", two_t)
-
-        neg_gt = keep.tile([P, PACK], F32, name="neg_gt")
-        nc.scalar.mul(neg_gt[:], gt_t[:], -1.0)
+            lo = HALF if t == 0 else 0
+            product(a_banks[t][:, lo:], xa_codes[:, cols], xa_scales[:, cols], wa_op[0][:, lo:], wa_op[1][:, lo:])
+        xb_codes = pick_words("xb_codes", two_t, "wa_raw384")
+        wb_op = operand_tiles("wb")
+        quantise_piece(wb_op, WB_PIECES[0], group_piece("wb_grouped0", on_vector, wb_raw[0][:]))
 
         z_planes = keep.tile([P, PACK, H], BF16, name="z_planes", align_bytes=64)
         z2_planes = keep.tile([P, PACK, N], BF16, name="z2_planes", align_bytes=64)
 
         def mix(t):
-            nc.scalar.copy(rows[t][:, :H], a_banks[t][:])
+            first = HALF if t == 0 else 0
+            nc.scalar.copy(rows[t][:, first:H], a_banks[t][:, first:])
             gate = keep.tile([P, H], F32, name=f"gate{t}")
-            nc.scalar.activation(gate[:], rows[t][:].indirect(n2_t[:]), ACT.Sigmoid)
+            far = keep.tile([P, H], F32, name=f"far{t}")
+            for lo, hi in WB_PIECES if t == 0 else ((0, H),):
+                nc.scalar.activation(gate[:, lo:hi], rows[t][:].indirect(n2_t[:, lo // 16 : hi // 16]), ACT.Sigmoid)
+                nc.vector.tensor_tensor(
+                    far[:, lo:hi], rows[t][:].indirect(n3_t[:, lo // 16 : hi // 16]), gate[:, lo:hi], ALU.mult
+                )
             rest = keep.tile([P, H], F32, name=f"rest{t}")
             nc.scalar.activation(
                 rest[:], gate[:], ACT.Identity, bias=gt_t[:, t : t + 1], scale=neg_gt[:, t : t + 1]
             )
-            far = keep.tile([P, H], F32, name=f"far{t}")
-            nc.vector.tensor_tensor(far[:], rows[t][:].indirect(n3_t[:]), gate[:], ALU.mult)
             near = keep.tile([P, H], F32, name=f"near{t}")
             nc.vector.tensor_tensor(near[:], rows[t][:].indirect(n1_t[:]), rest[:], ALU.mult)
             return far, near
 
         def join(t, far, near):
             nc.vector.scalar_tensor_tensor(
-                z_planes[:, t, :].rearrange("p (u m) -> p m u", u=PACK),
-                far[:].rearrange("p (m u) -> p m u", u=PACK),
+                z_planes[:, t, :],
+                far[:],
                 gt_t[:, t : t + 1],
-                near[:].rearrange("p (m u) -> p m u", u=PACK),
+                near[:],
                 ALU.mult,
                 ALU.add,
             )
 
         parts0 = mix(0)
-        parts1 = mix(1)
+        wb_grouped1 = group_piece("wb_grouped1", on_vector, wb_raw[1][:])
         join(0, *parts0)
-        wb_codes, wb_scales = weight_operand("wb", wb_raw)
-        b_banks = [psum.tile([P, N], F32, name=f"b_bank{t}") for t in range(PACK)]
+        quantise_piece(wb_op, WB_PIECES[1], wb_grouped1)
+        b_banks = [psum.tile([P, N], F32, name=f"b_bank{t}", tag=f"bank{PACK + t}") for t in range(PACK)]
         for t in range(PACK):
             cols = slice(t * P, (t + 1) * P)
-            product(b_banks[t][:], xb_codes[:, cols], xb_scales[:, cols], wb_codes[:], wb_scales[:])
+            product(b_banks[t][:], xb_codes[:, cols], xb_scales[:, cols], wb_op[0][:], wb_op[1][:])
+        parts1 = mix(1)
         parts2 = mix(2)
         join(1, *parts1)
         parts3 = mix(3)
         join(2, *parts2)
         for t in range(PACK):
             nc.scalar.activation(z2_planes[:, t, :], b_banks[t][:], ACT.Copy, scale=gi_t[:, t : t + 1])
-        z2_grouped = keep.tile([P, PACK * N], BF16, name="z2_grouped", align_bytes=64)
-        interleave(nc.vector.tensor_copy, z2_grouped[:], z2_planes[:])
         join(3, *parts3)
-        z2_codes = keep.tile([P, N], U32, name="z2_codes", align_bytes=64)
-        z2_scales = keep.tile([P, N], U8, name="z2_scales", align_bytes=64)
-        quantise(z2_codes[:], z2_scales[:], z2_grouped[:])
+        z2_op = operand_tiles("z2")
+        for i, (lo, hi) in enumerate(WB_PIECES):
+            quantise_piece(z2_op, (lo, hi), group_piece(f"z2_grouped{i}", on_scalar, z2_planes[:, :, lo:hi]))
+        z2_codes, z2_scales = z2_op
 
         z_grouped = [keep.tile([P, PACK * P], BF16, name=f"z_grouped{u}", align_bytes=64) for u in range(PACK)]
         z_codes = [keep.tile([P, P], U32, name=f"z_codes{u}", align_bytes=64) for u in range(PACK)]
@@ -186,7 +223,11 @@ def tile_picked_momlerpgmax_none_p_kernel(
         cv_banks = [psum.tile([P, N], F32, name=f"cv_bank{u}", tag=f"bank{u}") for u in range(PACK)]
         for u in range(PACK + 1):
             if u < PACK:
-                interleave(nc.vector.tensor_copy, z_grouped[u][:], z_planes[:, :, u * P : (u + 1) * P])
+                copy = on_vector
+                copy(
+                    z_grouped[u][:].rearrange("p (c i t) -> p c t i", i=2, t=PACK),
+                    z_planes[:].rearrange("p t (c i u) -> p u c t i", i=2, u=PACK)[:, u],
+                )
             if u > 0:
                 quantise(z_codes[u - 1][:], z_scales[u - 1][:], z_grouped[u - 1][:])
                 product(cv_banks[u - 1][:], z_codes[u - 1][:], z_scales[u - 1][:], z2_codes[:], z2_scales[:])
@@ -203,8 +244,9 @@ def tile_picked_momlerpgmax_none_p_kernel(
                 nc.vector.tensor_copy(other[u][:], rows[u][:].indirect(n5_t[:]))
             if u > 0:
                 result = keep.tile([P, N], F32, name=f"result{u - 1}")
-                nc.vector.tensor_tensor(result[:], gated[u - 1][:], other[u - 1][:], ALU.max)
-                nc.sync.dma_start(out_rows[:, u - 1, :], result[:])
+                for lo, hi in WB_PIECES if u == PACK else ((0, N),):
+                    nc.vector.tensor_tensor(result[:, lo:hi], gated[u - 1][:, lo:hi], other[u - 1][:, lo:hi], ALU.max)
+                    nc.sync.dma_start(out_rows[:, u - 1, lo:hi], result[:, lo:hi])
             if u < PACK:
                 gated.append(keep.tile([P, N], F32, name=f"gated{u}"))
                 nc.vector.tensor_tensor(gated[u][:], rows[u][:, :N], gate[:], ALU.mult)

@@ -89,16 +89,16 @@ def tile_picked_momlerpgmax_none_p_kernel(
             nc.sync.dma_start(
                 plane[32 * q : 32 * q + 4, :].bitcast(I32), x_scales[0, 4 * q : 4 * q + 4, :].bitcast(I32)
             )
-        two_t = load_list("two_t", two)
         words = keep.tile([P, T], I32, name="words")
         nc.sync.dma_start(words[:], x_words[0].rearrange("p c r -> p (c r)").bitcast(I32))
+        two_t = load_list("two_t", two)
         wa_raw = load_weight("wa_raw", wa, WA_PIECES)
-        load_gain(0, gt)
-        load_gain(PACK, gi)
         n2_t = load_list("n2_t", n2)
+        wb_raw = load_weight("wb_raw", wb, WB_PIECES)
         n3_t = load_list("n3_t", n3)
         n1_t = load_list("n1_t", n1)
-        wb_raw = load_weight("wb_raw", wb, WB_PIECES)
+        load_gain(0, gt)
+        load_gain(PACK, gi)
         n5_t = load_list("n5_t", n5)
         n4_t = load_list("n4_t", n4)
 
@@ -138,20 +138,13 @@ def tile_picked_momlerpgmax_none_p_kernel(
         xb_scales = pick_scales("xb_scales", two_t)
         xa_codes = pick_words("xa_codes", offs_t, "xa_codes")
         wa_op = operand_tiles("wa")
-        wa_grouped = [
-            group_piece(f"wa_grouped{i}", copy, wa_raw[i][:]) for i, copy in enumerate((on_scalar, on_vector, on_vector))
-        ]
-        for piece, grouped in zip(WA_PIECES, wa_grouped):
+        wa_grouped = [keep.tile([P, PACK * HALF], BF16, name=f"wa_grouped{i}", align_bytes=64) for i in range(2)]
+        for raw, (lo, hi) in zip(wa_raw, WA_PIECES):
+            first = lo % HALF
+            interleave(on_scalar, wa_grouped[lo // HALF][:, PACK * first : PACK * (first + hi - lo)], raw[:])
+        xb_codes = pick_words("xb_codes", two_t, "xb_codes")
+        for piece, grouped in zip(WB_PIECES, wa_grouped):
             quantise_piece(wa_op, piece, grouped)
-
-        gain_bank = psum.tile([P, P], F32, name="gain_bank", tag="bank7")
-        nc.tensor.transpose(gain_bank[:], gain_rows[:], identity[:])
-        gains = keep.tile([P, 2 * PACK], F32, name="gains")
-        nc.scalar.copy(gains[:], gain_bank[:, : 2 * PACK])
-        neg_gt = keep.tile([P, PACK], F32, name="neg_gt")
-        nc.scalar.mul(neg_gt[:], gain_bank[:, :PACK], -1.0)
-        gt_t = gains[:, :PACK]
-        gi_t = gains[:, PACK:]
 
         a_first = psum.tile([P, HALF], F32, name="a_first", tag="bank4")
         product(a_first[:], xa_codes[:, :P], xa_scales[:, :P], wa_op[0][:, :HALF], wa_op[1][:, :HALF])
@@ -161,9 +154,19 @@ def tile_picked_momlerpgmax_none_p_kernel(
             cols = slice(t * P, (t + 1) * P)
             lo = HALF if t == 0 else 0
             product(a_banks[t][:, lo:], xa_codes[:, cols], xa_scales[:, cols], wa_op[0][:, lo:], wa_op[1][:, lo:])
-        xb_codes = pick_words("xb_codes", two_t, "wa_raw384")
+        gain_bank = psum.tile([P, P], F32, name="gain_bank", tag="bank7")
+        nc.tensor.transpose(gain_bank[:], gain_rows[:], identity[:])
+        gains = keep.tile([P, 2 * PACK], F32, name="gains")
+        nc.scalar.copy(gains[:], gain_bank[:, : 2 * PACK])
+        neg_gt = keep.tile([P, PACK], F32, name="neg_gt")
+        nc.scalar.mul(neg_gt[:], gain_bank[:, :PACK], -1.0)
+        gt_t = gains[:, :PACK]
+        gi_t = gains[:, PACK:]
+
         wb_op = operand_tiles("wb")
-        quantise_piece(wb_op, WB_PIECES[0], group_piece("wb_grouped0", on_vector, wb_raw[0][:]))
+        wb_grouped = [group_piece(f"wb_grouped{i}", on_vector, wb_raw[i][:]) for i in range(2)]
+        for piece, grouped in zip(WB_PIECES, wb_grouped):
+            quantise_piece(wb_op, piece, grouped)
 
         z_planes = keep.tile([P, PACK, H], BF16, name="z_planes", align_bytes=64)
         z2_planes = keep.tile([P, PACK, N], BF16, name="z2_planes", align_bytes=64)
@@ -197,14 +200,12 @@ def tile_picked_momlerpgmax_none_p_kernel(
             )
 
         parts0 = mix(0)
-        wb_grouped1 = group_piece("wb_grouped1", on_vector, wb_raw[1][:])
-        join(0, *parts0)
-        quantise_piece(wb_op, WB_PIECES[1], wb_grouped1)
         b_banks = [psum.tile([P, N], F32, name=f"b_bank{t}", tag=f"bank{PACK + t}") for t in range(PACK)]
         for t in range(PACK):
             cols = slice(t * P, (t + 1) * P)
             product(b_banks[t][:], xb_codes[:, cols], xb_scales[:, cols], wb_op[0][:], wb_op[1][:])
         parts1 = mix(1)
+        join(0, *parts0)
         parts2 = mix(2)
         join(1, *parts1)
         parts3 = mix(3)
@@ -213,40 +214,58 @@ def tile_picked_momlerpgmax_none_p_kernel(
             nc.scalar.activation(z2_planes[:, t, :], b_banks[t][:], ACT.Copy, scale=gi_t[:, t : t + 1])
         join(3, *parts3)
         z2_op = operand_tiles("z2")
-        for i, (lo, hi) in enumerate(WB_PIECES):
-            quantise_piece(z2_op, (lo, hi), group_piece(f"z2_grouped{i}", on_scalar, z2_planes[:, :, lo:hi]))
+        z2_grouped = [
+            keep.tile([P, PACK * HALF], BF16, name="z2_grouped0", align_bytes=64),
+            keep.tile([P, PACK * HALF], BF16, name="z2_grouped1", tag="grouped", align_bytes=64),
+        ]
+        for (lo, hi), grouped, copy in zip(WB_PIECES, z2_grouped, (on_scalar, on_scalar)):
+            interleave(copy, grouped[:], z2_planes[:, :, lo:hi])
+        for piece, grouped in zip(WB_PIECES, z2_grouped):
+            quantise_piece(z2_op, piece, grouped)
         z2_codes, z2_scales = z2_op
 
-        z_grouped = [keep.tile([P, PACK * P], BF16, name=f"z_grouped{u}", align_bytes=64) for u in range(PACK)]
+        z_grouped = [
+            keep.tile([P, PACK * P], BF16, name=f"z_grouped{u}", tag="grouped" if u == 3 else f"z_grouped{u}", align_bytes=64)
+            for u in range(PACK)
+        ]
         z_codes = [keep.tile([P, P], U32, name=f"z_codes{u}", align_bytes=64) for u in range(PACK)]
         z_scales = [keep.tile([P, P], U8, name=f"z_scales{u}", align_bytes=64) for u in range(PACK)]
+        cv_first = psum.tile([P, HALF], F32, name="cv_first", tag="bank4")
         cv_banks = [psum.tile([P, N], F32, name=f"cv_bank{u}", tag=f"bank{u}") for u in range(PACK)]
-        for u in range(PACK + 1):
-            if u < PACK:
-                copy = on_vector
-                copy(
-                    z_grouped[u][:].rearrange("p (c i t) -> p c t i", i=2, t=PACK),
-                    z_planes[:].rearrange("p t (c i u) -> p u c t i", i=2, u=PACK)[:, u],
-                )
-            if u > 0:
-                quantise(z_codes[u - 1][:], z_scales[u - 1][:], z_grouped[u - 1][:])
-                product(cv_banks[u - 1][:], z_codes[u - 1][:], z_scales[u - 1][:], z2_codes[:], z2_scales[:])
+        for u, copy in enumerate((on_vector, on_scalar, on_scalar, on_vector)):
+            copy(
+                z_grouped[u][:].rearrange("p (c i t) -> p c t i", i=2, t=PACK),
+                z_planes[:].rearrange("p t (c i u) -> p u c t i", i=2, u=PACK)[:, u],
+            )
+        for u in range(PACK):
+            quantise(z_codes[u][:], z_scales[u][:], z_grouped[u][:])
+            first = HALF if u == 0 else 0
+            if u == 0:
+                product(cv_first[:], z_codes[u][:], z_scales[u][:], z2_codes[:, :HALF], z2_scales[:, :HALF])
+            product(cv_banks[u][:, first:], z_codes[u][:], z_scales[u][:], z2_codes[:, first:], z2_scales[:, first:])
 
         out_rows = out.rearrange("(p u) n -> p u n", u=PACK)
         gated = []
         other = []
-        for u in range(PACK + 1):
-            if u < PACK:
+
+        def finish(u, pieces):
+            result = keep.tile([P, N], F32, name=f"result{u}")
+            for lo, hi in pieces:
+                nc.vector.tensor_tensor(result[:, lo:hi], gated[u][:, lo:hi], other[u][:, lo:hi], ALU.max)
+                nc.sync.dma_start(out_rows[:, u, lo:hi], result[:, lo:hi])
+
+        for u in range(PACK):
+            if u == 0:
+                nc.scalar.activation(rows[u][:, :HALF], cv_first[:], ACT.Copy, scale=0.0625)
+                nc.vector.tensor_scalar(rows[u][:, HALF:N], cv_banks[u][:, HALF:], 0.0625, None, ALU.mult)
+            else:
                 nc.scalar.activation(rows[u][:, :N], cv_banks[u][:], ACT.Copy, scale=0.0625)
-                gate = keep.tile([P, N], F32, name=f"cv_gate{u}")
-                nc.scalar.activation(gate[:], rows[u][:].indirect(n4_t[:]), ACT.Sigmoid)
-                other.append(keep.tile([P, N], F32, name=f"other{u}"))
-                nc.vector.tensor_copy(other[u][:], rows[u][:].indirect(n5_t[:]))
+            gate = keep.tile([P, N], F32, name=f"cv_gate{u}")
+            nc.scalar.activation(gate[:], rows[u][:].indirect(n4_t[:]), ACT.Sigmoid)
+            other.append(keep.tile([P, N], F32, name=f"other{u}"))
+            nc.vector.tensor_copy(other[u][:], rows[u][:].indirect(n5_t[:]))
+            gated.append(keep.tile([P, N], F32, name=f"gated{u}"))
+            nc.vector.tensor_tensor(gated[u][:], rows[u][:, :N], gate[:], ALU.mult)
             if u > 0:
-                result = keep.tile([P, N], F32, name=f"result{u - 1}")
-                for lo, hi in WB_PIECES if u == PACK else ((0, N),):
-                    nc.vector.tensor_tensor(result[:, lo:hi], gated[u - 1][:, lo:hi], other[u - 1][:, lo:hi], ALU.max)
-                    nc.sync.dma_start(out_rows[:, u - 1, lo:hi], result[:, lo:hi])
-            if u < PACK:
-                gated.append(keep.tile([P, N], F32, name=f"gated{u}"))
-                nc.vector.tensor_tensor(gated[u][:], rows[u][:, :N], gate[:], ALU.mult)
+                finish(u - 1, ((0, N),))
+        finish(PACK - 1, WB_PIECES)

@@ -1,7 +1,6 @@
 from contextlib import ExitStack
 
 import concourse.mybir as mybir
-from concourse.masks import make_identity
 
 K, T, S, H, N = 512, 2048, 512, 512, 512
 FLOPS = 2 * K * S * H + 2 * K * S * N + 2 * S * H * N
@@ -44,11 +43,10 @@ def tile_picked_momlerpgmax_none_p_kernel(
                 raws.append(raw)
             return raws
 
-        def load_gain(first_row, g):
-            nc.sync.dma_start(
-                gain_rows[first_row : first_row + PACK, :].rearrange("t (b q) -> t b q", q=8),
-                g.rearrange("(b t q) o -> t b (q o)", t=PACK, q=8),
-            )
+        def load_gain(name, g):
+            tile = keep.tile([P, PACK], F32, name=name)
+            nc.sync.dma_start(tile[:], g.rearrange("(p t) o -> p (t o)", t=PACK))
+            return tile
 
         def interleave(copy, dst, src):
             copy(
@@ -76,10 +74,6 @@ def tile_picked_momlerpgmax_none_p_kernel(
         warm_out = keep.tile([P, 1], F32, name="warm_out")
         nc.gpsimd.memset(warm[:], 0.0)
         nc.scalar.activation(warm_out[:], warm[:], ACT.Sigmoid)
-        gain_rows = keep.tile([P, P], F32, name="gain_rows")
-        nc.gpsimd.memset(gain_rows[:], 0.0)
-        identity = keep.tile([P, P], F32, name="identity")
-        make_identity(nc, identity[:])
         rows = [keep.tile([P, 2 * H], F32, name=f"rows{t}") for t in range(PACK)]
         for t in range(PACK):
             nc.vector.memset(rows[t][:, H:], 0.0)
@@ -89,16 +83,16 @@ def tile_picked_momlerpgmax_none_p_kernel(
             nc.sync.dma_start(
                 plane[32 * q : 32 * q + 4, :].bitcast(I32), x_scales[0, 4 * q : 4 * q + 4, :].bitcast(I32)
             )
+        two_t = load_list("two_t", two)
         words = keep.tile([P, T], I32, name="words")
         nc.sync.dma_start(words[:], x_words[0].rearrange("p c r -> p (c r)").bitcast(I32))
-        two_t = load_list("two_t", two)
         wa_raw = load_weight("wa_raw", wa, WA_PIECES)
         n2_t = load_list("n2_t", n2)
+        gt_t = load_gain("gt_t", gt)
         wb_raw = load_weight("wb_raw", wb, WB_PIECES)
         n3_t = load_list("n3_t", n3)
         n1_t = load_list("n1_t", n1)
-        load_gain(0, gt)
-        load_gain(PACK, gi)
+        gi_t = load_gain("gi_t", gi)
         n5_t = load_list("n5_t", n5)
         n4_t = load_list("n4_t", n4)
 
@@ -107,15 +101,14 @@ def tile_picked_momlerpgmax_none_p_kernel(
             nc.vector.tensor_copy(picked[:], plane[:].indirect(idx[:]))
             dealt = keep.tile([P, S], U8, name=name + "_dealt", align_bytes=64)
             nc.vector.tensor_copy(
-                dealt[:].bitcast(I32).rearrange("p (t b w) -> p t b w", t=PACK, w=2),
-                picked[:].bitcast(I32).rearrange("p (b t w) -> p t b w", t=PACK, w=2),
+                dealt[:].rearrange("p (t m) -> p m t", t=PACK), picked[:].rearrange("p (m t) -> p m t", t=PACK)
             )
             return dealt
 
         def pick_words(name, idx, tag):
             dealt = keep.tile([P, S], U32, name=name, tag=tag, align_bytes=64)
             nc.vector.tensor_copy(
-                dealt[:].rearrange("p (t b q) -> p b t q", t=PACK, q=8), words[:].bitcast(U32).indirect(idx[:])
+                dealt[:].rearrange("p (t m) -> p m t", t=PACK), words[:].bitcast(U32).indirect(idx[:])
             )
             return dealt
 
@@ -154,15 +147,8 @@ def tile_picked_momlerpgmax_none_p_kernel(
             cols = slice(t * P, (t + 1) * P)
             lo = HALF if t == 0 else 0
             product(a_banks[t][:, lo:], xa_codes[:, cols], xa_scales[:, cols], wa_op[0][:, lo:], wa_op[1][:, lo:])
-        gain_bank = psum.tile([P, P], F32, name="gain_bank", tag="bank7")
-        nc.tensor.transpose(gain_bank[:], gain_rows[:], identity[:])
-        gains = keep.tile([P, 2 * PACK], F32, name="gains")
-        nc.scalar.copy(gains[:], gain_bank[:, : 2 * PACK])
         neg_gt = keep.tile([P, PACK], F32, name="neg_gt")
-        nc.scalar.mul(neg_gt[:], gain_bank[:, :PACK], -1.0)
-        gt_t = gains[:, :PACK]
-        gi_t = gains[:, PACK:]
-
+        nc.scalar.mul(neg_gt[:], gt_t[:], -1.0)
         wb_op = operand_tiles("wb")
         wb_grouped = [group_piece(f"wb_grouped{i}", on_vector, wb_raw[i][:]) for i in range(2)]
         for piece, grouped in zip(WB_PIECES, wb_grouped):

@@ -131,13 +131,16 @@ def tile_picked_momlerpgmax_none_p_kernel(
         xb_scales = pick_scales("xb_scales", two_t)
         xa_codes = pick_words("xa_codes", offs_t, "xa_codes")
         wa_op = operand_tiles("wa")
-        wa_grouped = [keep.tile([P, PACK * HALF], BF16, name=f"wa_grouped{i}", align_bytes=64) for i in range(2)]
-        for raw, (lo, hi) in zip(wa_raw, WA_PIECES):
+        wa_grouped = [
+            keep.tile([P, PACK * HALF], BF16, name=f"wa_grouped{i}", tag=f"wa_grouped{i}", align_bytes=64)
+            for i in range(2)
+        ]
+        for raw, (lo, hi), copy in zip(wa_raw, WA_PIECES, (on_scalar, on_scalar, on_vector)):
             first = lo % HALF
-            interleave(on_scalar, wa_grouped[lo // HALF][:, PACK * first : PACK * (first + hi - lo)], raw[:])
-        xb_codes = pick_words("xb_codes", two_t, "xb_codes")
+            interleave(copy, wa_grouped[lo // HALF][:, PACK * first : PACK * (first + hi - lo)], raw[:])
         for piece, grouped in zip(WB_PIECES, wa_grouped):
             quantise_piece(wa_op, piece, grouped)
+        xb_codes = pick_words("xb_codes", two_t, "wa_grouped1")
 
         a_first = psum.tile([P, HALF], F32, name="a_first", tag="bank4")
         product(a_first[:], xa_codes[:, :P], xa_scales[:, :P], wa_op[0][:, :HALF], wa_op[1][:, :HALF])
@@ -150,7 +153,11 @@ def tile_picked_momlerpgmax_none_p_kernel(
         neg_gt = keep.tile([P, PACK], F32, name="neg_gt")
         nc.scalar.mul(neg_gt[:], gt_t[:], -1.0)
         wb_op = operand_tiles("wb")
-        wb_grouped = [group_piece(f"wb_grouped{i}", on_vector, wb_raw[i][:]) for i in range(2)]
+        wb_first = keep.tile([P, PACK * HALF], BF16, name="wb_first", align_bytes=64)
+        nc.gpsimd.tensor_copy(
+            wb_first[:].rearrange("p (c t) -> p c t", t=PACK), wb_raw[0][:].rearrange("p t c -> p c t")
+        )
+        wb_grouped = [wb_first, group_piece("wb_grouped1", on_vector, wb_raw[1][:])]
         for piece, grouped in zip(WB_PIECES, wb_grouped):
             quantise_piece(wb_op, piece, grouped)
 
@@ -251,7 +258,8 @@ def tile_picked_momlerpgmax_none_p_kernel(
             other.append(keep.tile([P, N], F32, name=f"other{u}"))
             nc.vector.tensor_copy(other[u][:], rows[u][:].indirect(n5_t[:]))
             gated.append(keep.tile([P, N], F32, name=f"gated{u}"))
-            nc.vector.tensor_tensor(gated[u][:], rows[u][:, :N], gate[:], ALU.mult)
+            engine = nc.gpsimd if u < 2 else nc.vector
+            engine.tensor_tensor(gated[u][:], rows[u][:, :N], gate[:], ALU.mult)
             if u > 0:
                 finish(u - 1, ((0, N),))
         finish(PACK - 1, WB_PIECES)

from contextlib import ExitStack

import concourse.mybir as mybir

K, T, S, H, N = 512, 2048, 512, 512, 512
FLOPS = 2 * K * S * H + 2 * K * S * N + 2 * S * H * N

F32 = mybir.dt.float32
BF16 = mybir.dt.bfloat16
I32 = mybir.dt.int32
U32 = mybir.dt.uint32
U16 = mybir.dt.uint16
U8 = mybir.dt.uint8
FP8X4 = mybir.dt.float8_e4m3fn_x4
ALU = mybir.AluOpType
ACT = mybir.ActivationFunctionType

P = 128
PACK = 4
HALF = 256
WA_PIECES = ((0, 256), (256, 384), (384, 512))
WB_PIECES = ((0, 256), (256, 512))


def tile_picked_momlerpgmax_none_p_kernel(
    tc, x_words, x_scales, wa, wb, gt, gi, offs, two, n1, n2, n3, n4, n5, out
):
    nc = tc.nc
    with ExitStack() as ctx:
        keep = ctx.enter_context(tc.tile_pool(name="keep", bufs=1))
        psum = ctx.enter_context(tc.psum_pool(name="psum", bufs=1))

        def load_list(name, src):
            tile = keep.tile([P, S // 16], U16, name=name)
            nc.sync.dma_start(tile[:], src)
            return tile

        def load_weight(name, w, pieces):
            raws = []
            for lo, hi in pieces:
                raw = keep.tile([P, PACK, hi - lo], F32, name=f"{name}{lo}", tag=f"{name}{lo}", align_bytes=64)
                nc.sync.dma_start(raw[:], w.rearrange("(p j) c -> p j c", j=PACK)[:, :, lo:hi])
                raws.append(raw)
            return raws

        def load_gain(name, g):
            tile = keep.tile([P, PACK], F32, name=name)
            nc.sync.dma_start(tile[:], g.rearrange("(p t) o -> p (t o)", t=PACK))
            return tile

        def interleave(copy, dst, src):
            copy(
                dst.rearrange("p (c i t) -> p c t i", i=4, t=PACK),
                src.rearrange("p t (c i) -> p c t i", i=4),
            )

        def quantise(codes, scales, grouped):
            nc.vector.quantize_mx(out=codes.bitcast(FP8X4), scales=scales, in_=grouped)

        def product(acc, l_codes, l_scales, r_codes, r_scales):
            nc.tensor.matmul_mx(
                out=acc,
                lhsT=l_codes.bitcast(FP8X4),
                lhsT_scale=l_scales,
                rhs=r_codes.bitcast(FP8X4),
                rhs_scale=r_scales,
                start=True,
                stop=True,
            )

        plane = keep.tile([P, T], U8, name="plane", align_bytes=64)
        nc.gpsimd.memset(plane[:].bitcast(I32), 0)
        warm = keep.tile([P, 1], F32, name="warm")
        warm_out = keep.tile([P, 1], F32, name="warm_out")
        nc.gpsimd.memset(warm[:], 0.0)
        nc.scalar.activation(warm_out[:], warm[:], ACT.Sigmoid)
        rows = [keep.tile([P, 2 * H], F32, name=f"rows{t}") for t in range(PACK)]
        for t in range(PACK):
            nc.vector.memset(rows[t][:, H:], 0.0)

        offs_t = load_list("offs_t", offs)
        for q in range(4):
            nc.sync.dma_start(
                plane[32 * q : 32 * q + 4, :].bitcast(I32), x_scales[0, 4 * q : 4 * q + 4, :].bitcast(I32)
            )
        two_t = load_list("two_t", two)
        words = keep.tile([P, T], I32, name="words")
        nc.sync.dma_start(words[:], x_words[0].rearrange("p c r -> p (c r)").bitcast(I32))
        wa_raw = load_weight("wa_raw", wa, WA_PIECES)
        n2_t = load_list("n2_t", n2)
        gt_t = load_gain("gt_t", gt)
        wb_raw = load_weight("wb_raw", wb, WB_PIECES)
        n3_t = load_list("n3_t", n3)
        n1_t = load_list("n1_t", n1)
        gi_t = load_gain("gi_t", gi)
        n5_t = load_list("n5_t", n5)
        n4_t = load_list("n4_t", n4)

        def pick_scales(name, idx):
            picked = keep.tile([P, S], U8, name=name + "_picked", align_bytes=64)
            nc.vector.tensor_copy(picked[:], plane[:].indirect(idx[:]))
            dealt = keep.tile([P, S], U8, name=name + "_dealt", align_bytes=64)
            nc.vector.tensor_copy(
                dealt[:].rearrange("p (t m) -> p m t", t=PACK), picked[:].rearrange("p (m t) -> p m t", t=PACK)
            )
            return dealt

        def pick_words(name, idx, tag):
            dealt = keep.tile([P, S], U32, name=name, tag=tag, align_bytes=64)
            nc.vector.tensor_copy(
                dealt[:].rearrange("p (t m) -> p m t", t=PACK), words[:].bitcast(U32).indirect(idx[:])
            )
            return dealt

        def operand_tiles(name):
            codes = keep.tile([P, H], U32, name=name + "_codes", align_bytes=64)
            scales = keep.tile([P, H], U8, name=name + "_scales", align_bytes=64)
            return codes, scales

        def group_piece(name, copy, source):
            grouped = keep.tile([P, PACK * source.shape[2]], BF16, name=name, align_bytes=64)
            interleave(copy, grouped[:], source)
            return grouped

        def quantise_piece(operand, piece, grouped):
            lo, hi = piece
            quantise(operand[0][:, lo:hi], operand[1][:, lo:hi], grouped[:])

        on_scalar, on_vector = nc.scalar.copy, nc.vector.tensor_copy
        xa_scales = pick_scales("xa_scales", offs_t)
        xb_scales = pick_scales("xb_scales", two_t)
        xa_codes = pick_words("xa_codes", offs_t, "xa_codes")
        wa_op = operand_tiles("wa")
        wa_grouped = [
            keep.tile([P, PACK * HALF], BF16, name=f"wa_grouped{i}", tag=f"wa_grouped{i}", align_bytes=64)
            for i in range(2)
        ]
        for raw, (lo, hi), copy in zip(wa_raw, WA_PIECES, (on_scalar, on_scalar, on_vector)):
            first = lo % HALF
            interleave(copy, wa_grouped[lo // HALF][:, PACK * first : PACK * (first + hi - lo)], raw[:])
        for piece, grouped in zip(WB_PIECES, wa_grouped):
            quantise_piece(wa_op, piece, grouped)
        xb_codes = pick_words("xb_codes", two_t, "wa_grouped1")

        a_first = psum.tile([P, HALF], F32, name="a_first", tag="bank4")
        product(a_first[:], xa_codes[:, :P], xa_scales[:, :P], wa_op[0][:, :HALF], wa_op[1][:, :HALF])
        nc.scalar.copy(rows[0][:, :HALF], a_first[:])
        a_banks = [psum.tile([P, H], F32, name=f"a_bank{t}", tag=f"bank{t}") for t in range(PACK)]
        for t in range(PACK):
            cols = slice(t * P, (t + 1) * P)
            lo = HALF if t == 0 else 0
            product(a_banks[t][:, lo:], xa_codes[:, cols], xa_scales[:, cols], wa_op[0][:, lo:], wa_op[1][:, lo:])
        neg_gt = keep.tile([P, PACK], F32, name="neg_gt")
        nc.scalar.mul(neg_gt[:], gt_t[:], -1.0)
        wb_op = operand_tiles("wb")
        wb_first = keep.tile([P, PACK * HALF], BF16, name="wb_first", align_bytes=64)
        nc.gpsimd.tensor_copy(
            wb_first[:].rearrange("p (c t) -> p c t", t=PACK), wb_raw[0][:].rearrange("p t c -> p c t")
        )
        wb_grouped = [wb_first, group_piece("wb_grouped1", on_vector, wb_raw[1][:])]
        for piece, grouped in zip(WB_PIECES, wb_grouped):
            quantise_piece(wb_op, piece, grouped)

        z_planes = keep.tile([P, PACK, H], BF16, name="z_planes", align_bytes=64)
        z2_planes = keep.tile([P, PACK, N], BF16, name="z2_planes", align_bytes=64)

        def mix(t):
            first = HALF if t == 0 else 0
            nc.scalar.copy(rows[t][:, first:H], a_banks[t][:, first:])
            gate = keep.tile([P, H], F32, name=f"gate{t}")
            far = keep.tile([P, H], F32, name=f"far{t}")
            for lo, hi in WB_PIECES if t == 0 else ((0, H),):
                nc.scalar.activation(gate[:, lo:hi], rows[t][:].indirect(n2_t[:, lo // 16 : hi // 16]), ACT.Sigmoid)
                nc.vector.tensor_tensor(
                    far[:, lo:hi], rows[t][:].indirect(n3_t[:, lo // 16 : hi // 16]), gate[:, lo:hi], ALU.mult
                )
            rest = keep.tile([P, H], F32, name=f"rest{t}")
            nc.scalar.activation(
                rest[:], gate[:], ACT.Identity, bias=gt_t[:, t : t + 1], scale=neg_gt[:, t : t + 1]
            )
            near = keep.tile([P, H], F32, name=f"near{t}")
            nc.vector.tensor_tensor(near[:], rows[t][:].indirect(n1_t[:]), rest[:], ALU.mult)
            return far, near

        def join(t, far, near):
            nc.vector.scalar_tensor_tensor(
                z_planes[:, t, :],
                far[:],
                gt_t[:, t : t + 1],
                near[:],
                ALU.mult,
                ALU.add,
            )

        parts0 = mix(0)
        b_banks = [psum.tile([P, N], F32, name=f"b_bank{t}", tag=f"bank{PACK + t}") for t in range(PACK)]
        for t in range(PACK):
            cols = slice(t * P, (t + 1) * P)
            product(b_banks[t][:], xb_codes[:, cols], xb_scales[:, cols], wb_op[0][:], wb_op[1][:])
        parts1 = mix(1)
        join(0, *parts0)
        parts2 = mix(2)
        join(1, *parts1)
        parts3 = mix(3)
        join(2, *parts2)
        for t in range(PACK):
            nc.scalar.activation(z2_planes[:, t, :], b_banks[t][:], ACT.Copy, scale=gi_t[:, t : t + 1])
        join(3, *parts3)
        z2_op = operand_tiles("z2")
        z2_grouped = [
            keep.tile([P, PACK * HALF], BF16, name="z2_grouped0", align_bytes=64),
            keep.tile([P, PACK * HALF], BF16, name="z2_grouped1", tag="grouped", align_bytes=64),
        ]
        for (lo, hi), grouped, copy in zip(WB_PIECES, z2_grouped, (on_scalar, on_scalar)):
            interleave(copy, grouped[:], z2_planes[:, :, lo:hi])
        for piece, grouped in zip(WB_PIECES, z2_grouped):
            quantise_piece(z2_op, piece, grouped)
        z2_codes, z2_scales = z2_op

        z_grouped = [
            keep.tile([P, PACK * P], BF16, name=f"z_grouped{u}", tag="grouped" if u == 3 else f"z_grouped{u}", align_bytes=64)
            for u in range(PACK)
        ]
        z_codes = [keep.tile([P, P], U32, name=f"z_codes{u}", align_bytes=64) for u in range(PACK)]
        z_scales = [keep.tile([P, P], U8, name=f"z_scales{u}", align_bytes=64) for u in range(PACK)]
        cv_first = psum.tile([P, HALF], F32, name="cv_first", tag="bank4")
        cv_banks = [psum.tile([P, N], F32, name=f"cv_bank{u}", tag=f"bank{u}") for u in range(PACK)]
        for u, copy in enumerate((on_vector, on_scalar, on_scalar, on_vector)):
            copy(
                z_grouped[u][:].rearrange("p (c i t) -> p c t i", i=2, t=PACK),
                z_planes[:].rearrange("p t (c i u) -> p u c t i", i=2, u=PACK)[:, u],
            )
        for u in range(PACK):
            quantise(z_codes[u][:], z_scales[u][:], z_grouped[u][:])
            first = HALF if u == 0 else 0
            if u == 0:
                product(cv_first[:], z_codes[u][:], z_scales[u][:], z2_codes[:, :HALF], z2_scales[:, :HALF])
            product(cv_banks[u][:, first:], z_codes[u][:], z_scales[u][:], z2_codes[:, first:], z2_scales[:, first:])

        out_rows = out.rearrange("(p u) n -> p u n", u=PACK)
        gated = []
        other = []

        def finish(u, pieces):
            result = keep.tile([P, N], F32, name=f"result{u}")
            for lo, hi in pieces:
                nc.vector.tensor_tensor(result[:, lo:hi], gated[u][:, lo:hi], other[u][:, lo:hi], ALU.max)
                nc.sync.dma_start(out_rows[:, u, lo:hi], result[:, lo:hi])

        for u in range(PACK):
            if u == 0:
                nc.scalar.activation(rows[u][:, :HALF], cv_first[:], ACT.Copy, scale=0.0625)
                nc.vector.tensor_scalar(rows[u][:, HALF:N], cv_banks[u][:, HALF:], 0.0625, None, ALU.mult)
            else:
                nc.scalar.activation(rows[u][:, :N], cv_banks[u][:], ACT.Copy, scale=0.0625)
            gate = keep.tile([P, N], F32, name=f"cv_gate{u}")
            nc.scalar.activation(gate[:], rows[u][:].indirect(n4_t[:]), ACT.Sigmoid)
            other.append(keep.tile([P, N], F32, name=f"other{u}"))
            nc.vector.tensor_copy(other[u][:], rows[u][:].indirect(n5_t[:]))
            gated.append(keep.tile([P, N], F32, name=f"gated{u}"))
            engine = nc.gpsimd if u < 2 else nc.vector
            engine.tensor_tensor(gated[u][:], rows[u][:, :N], gate[:], ALU.mult)
            if u > 0:
                finish(u - 1, ((0, N),))
        finish(PACK - 1, WB_PIECES)
